import numpy as np
import ml_dtypes


def mxq(x, axis, fmt="e4m3"):
    dtype, down = {"e4m3": (ml_dtypes.float8_e4m3fn, 7), "e5m2": (ml_dtypes.float8_e5m2, 14)}[fmt]
    v = np.moveaxis(np.asarray(x, np.float32).astype(ml_dtypes.bfloat16).astype(np.float64), axis, -1)
    blocks = v.reshape(v.shape[:-1] + (-1, 32))
    amax = np.abs(blocks).max(-1, keepdims=True)
    byte = np.maximum(np.where(amax > 0, np.frexp(amax)[1] - 1 + 127, 0) - down, 1)
    scale = np.exp2(byte - 127.0)
    codes = (blocks / scale).astype(np.float32).astype(dtype).astype(np.float64)
    return np.moveaxis((codes * scale).reshape(v.shape), -1, axis)


WIDE = False


def mx_kscale(k):
    if not WIDE:
        return np.ones(k)
    levels = np.array([10, -10, 5, -5, 0])
    if k % 512:
        return np.exp2(np.random.permutation(np.resize(levels, k // 32))).repeat(32)
    a = np.empty((k // 512, 16))
    for p in range(k // 512):
        a[p, :8] = np.random.permutation(np.resize(levels, 8))
        for g in range(8):
            far = levels[np.abs(levels - a[p, g]) >= 10]
            a[p, g + 8] = far[np.random.randint(len(far))]
    return np.exp2(a.ravel()).repeat(32)


BF16 = ml_dtypes.bfloat16


def bf(x):
    return np.asarray(x, np.float32).astype(BF16)


def f64(x):
    return np.asarray(x).astype(np.float64)


E2M1 = np.array([0.0, 0.5, 1.0, 1.5, 2.0, 3.0, 4.0, 6.0, -0.0, -0.5, -1.0, -1.5, -2.0, -3.0, -4.0, -6.0])


def pack_weight(w, fmt):
    k, n = w.shape
    w = f64(bf(w)).reshape(k // 32, 32, n)
    amax = np.abs(w).max(1)
    if fmt == "e4m3":
        byte = np.frexp(amax)[1] - 1 + 127 - 7
    else:
        mant, ex = np.frexp(amax / 6.0)
        byte = np.where(mant > 0.5, ex, ex - 1) + 127
    byte = np.clip(np.where(amax > 0, byte, 1), 1, 254)
    scaled = (w * np.exp2(127.0 - byte)[:, None, :]).reshape(k, n).astype(np.float32)
    by_word = np.ascontiguousarray(scaled.reshape(k // 512, 128, 4, n).transpose(0, 1, 3, 2))
    if fmt == "e4m3":
        words = by_word.astype(ml_dtypes.float8_e4m3fn).view(np.uint8)
    else:
        c = by_word.astype(ml_dtypes.float4_e2m1fn).view(np.uint8) & 0xF
        words = c[..., 0::2] | (c[..., 1::2] << 4)
    return np.ascontiguousarray(words), np.ascontiguousarray(byte.astype(np.uint8).reshape(k // 512, 16, n))


def unpack_weight(words, scales, fmt):
    g, p, n, _ = words.shape
    if fmt == "e4m3":
        vals = np.ascontiguousarray(words).view(ml_dtypes.float8_e4m3fn).astype(np.float64)
    else:
        nib = np.empty((g, p, n, 4), np.uint8)
        nib[..., 0::2] = words & 0xF
        nib[..., 1::2] = words >> 4
        vals = E2M1[nib]
    vals = vals * np.repeat(np.exp2(scales.astype(np.float64) - 127.0), 8, axis=1)[..., None]
    return vals.transpose(0, 1, 3, 2).reshape(g * 512, n)
def pack4(w):
    words, scales = pack_weight(w, "e2m1")
    return words.reshape(words.shape[0], 128, -1), scales


def unpack4(words, scales):
    return unpack_weight(words.reshape(words.shape[0], 128, -1, 2), scales, "e2m1")


M, K, V, T = 2048, 1024, 3072, 512


def draw0():
    s = mx_kscale(K)
    u = mx_kscale(M)
    z = np.random.standard_normal((M, V)) / np.sqrt(M) / u[:, None]
    geno_words, geno_scales = pack4(z)
    return {
        "pred": bf(np.random.standard_normal((M, K)) * s * u[:, None]),
        "eff": bf(np.random.standard_normal((K, T)) / np.sqrt(K) / s[:, None]),
        "traits": bf(np.random.standard_normal((M, T)) * u[:, None]),
        "geno_words": geno_words,
        "geno_scales": geno_scales,
        "var": bf(np.exp(0.3 * np.random.standard_normal(V))),
    }


def core(pred, eff, traits, geno_words, geno_scales, var):
    fit = mxq(f64(pred), 1, "e4m3") @ mxq(f64(eff), 0, "e4m3")
    resid = f64(traits) - fit
    z = unpack4(geno_words, geno_scales)
    score = z.T @ mxq(resid, 0, "e4m3")
    return np.square(score) / f64(var)[:, None]


def e4m3fn_bytes(y):
    return np.clip(np.asarray(y, np.float64), -448.0, 448.0).astype(np.float32).astype(ml_dtypes.float8_e4m3fn).view(np.uint8)


def e4m3fn_values(b):
    return np.asarray(b, np.uint8).view(ml_dtypes.float8_e4m3fn).astype(np.float64)


def setup_inputs():
    d = draw0()
    x0 = np.asarray(d['eff']).astype(np.float64)
    s = (np.max(np.abs(x0), axis=(1,), keepdims=True) / 448.0).astype(np.float32)
    out = {}
    for k, v in d.items():
        if k == 'eff':
            out['eff_bytes'] = e4m3fn_bytes(x0 / s.astype(np.float64))
            out['eff_scale'] = s
        else:
            out[k] = v
    return out


def reference(pred, eff_bytes, eff_scale, traits, geno_words, geno_scales, var):
    return core(pred, e4m3fn_values(eff_bytes) * eff_scale.astype(np.float64), traits, geno_words, geno_scales, var)

@@ -1,0 +1,348 @@
+from contextlib import ExitStack
+
+import concourse.mybir as mybir
+from concourse.masks import make_identity
+
+INDIV, PRED, VARIANTS, TRAITS = 2048, 1024, 3072, 512
+FLOPS = 2 * INDIV * PRED * TRAITS + 2 * INDIV * VARIANTS * TRAITS
+
+F32 = mybir.dt.float32
+BF16 = mybir.dt.bfloat16
+I32 = mybir.dt.int32
+U32 = mybir.dt.uint32
+U8 = mybir.dt.uint8
+FP8 = mybir.dt.float8_e4m3fn
+FP8X4 = mybir.dt.float8_e4m3fn_x4
+FP4X4 = mybir.dt.float4_e2m1fn_x4
+ACT = mybir.ActivationFunctionType
+ALU = mybir.AluOpType
+
+P = 128
+PACK = 4
+K_PASS = P * PACK
+G = INDIV // K_PASS
+H = PRED // K_PASS
+C = TRAITS // P
+NV = VARIANTS // P
+HALF = TRAITS // 2
+FIRST = 6
+W_CHUNKS = ((0, 6), (6, 12), (12, 18), (18, 24))
+
+
+def tile_gwas_score_statistics_s13_kernel(
+    tc, pred, eff_bytes, eff_scale, traits, geno_words, geno_scales, var, out
+):
+    nc = tc.nc
+    with ExitStack() as ctx:
+        keep = ctx.enter_context(tc.tile_pool(name="keep", bufs=1))
+        work = ctx.enter_context(tc.tile_pool(name="work", bufs=3))
+        psum = ctx.enter_context(tc.psum_pool(name="psum", bufs=2))
+        ctx.enter_context(tc.manual_schedule())
+
+        ident = keep.tile([P, P], F32, name="ident")
+        make_identity(nc, ident[:])
+        ident_b = keep.tile([P, P], BF16, name="ident_b")
+        make_identity(nc, ident_b[:])
+        var_rows = keep.tile([P, P], BF16, name="var_rows")
+        nc.gpsimd.memset(var_rows[:], 0.0)
+        g_scales = keep.tile([P, G * VARIANTS], U8, name="g_scales", align_bytes=64)
+        nc.gpsimd.memset(g_scales[:].bitcast(I32), 0)
+        one = keep.tile([P, 1], F32, name="one")
+        nc.vector.memset(one[:], 1.0)
+        root = keep.tile([P, 1], F32, name="root")
+        nc.scalar.activation(out=root[:], in_=one[:], func=ACT.Sqrt)
+
+        e_scale = keep.tile([P, H * PACK], F32, name="e_scale")
+        nc.scalar.dma_start(
+            out=e_scale[:].rearrange("p (h t) -> p h t", h=H),
+            in_=eff_scale.rearrange("(h p t) o -> p h (t o)", p=P, t=PACK),
+        )
+        nc.scalar.dma_start(out=var_rows[0:NV, :], in_=var.rearrange("(j p) -> j p", p=P))
+
+        e_bytes = []
+        for h in range(H):
+            eb = keep.tile([P, PACK * TRAITS], U8, name="e_bytes%d" % h, align_bytes=64)
+            nc.sync.dma_start(
+                out=eb[:], in_=eff_bytes.rearrange("(h p t) n -> h p (t n)", p=P, t=PACK)[h]
+            )
+            e_bytes.append(eb)
+
+        pred_v = pred.rearrange("(g p t) k -> g p t k", p=P, t=PACK)
+        traits_v = traits.rearrange("(g p t) n -> g p t n", p=P, t=PACK)
+        p_raw, t_raw = [], []
+        for g in range(G):
+            pr = keep.tile([P, PACK, PRED], BF16, name="p_raw%d" % g, align_bytes=64)
+            p_raw.append(pr)
+            tr = keep.tile([P, PACK, TRAITS], BF16, name="t_raw%d" % g, align_bytes=64)
+            t_raw.append(tr)
+
+        def load_pred(g, t0, t1):
+            nc.sync.dma_start(out=p_raw[g][:, t0:t1, :], in_=pred_v[g, :, t0:t1, :])
+
+        def load_traits(g):
+            nc.sync.dma_start(out=t_raw[g][:], in_=traits_v[g])
+
+        g_words = keep.tile([P, G, 2 * VARIANTS], U8, name="g_words", align_bytes=64)
+        words_v = geno_words.bitcast(I32)
+        words_flat = g_words[:].rearrange("p g n -> p (g n)").bitcast(I32)
+        words_sb = words_flat.rearrange("p (g n) -> p g n", g=G)
+        scales_v = geno_scales.bitcast(I32)
+        scales_sb = g_scales[:].bitcast(I32).rearrange("p (g n) -> p g n", g=G)
+
+        def load_words(v0, v1):
+            cols = slice(v0 * P // 2, v1 * P // 2)
+            nc.sync.dma_start(
+                out=words_sb[:, :, cols], in_=words_v[:, :, cols].rearrange("g p n -> p g n")
+            )
+
+        def load_scales(q):
+            nc.sync.dma_start(
+                out=scales_sb[32 * q : 32 * q + 4, :, :],
+                in_=scales_v[:, 4 * q : 4 * q + 4, :].rearrange("g q n -> q g n"),
+            )
+
+        load_pred(0, 0, 1)
+        load_pred(0, 1, 2)
+        load_pred(0, 2, 4)
+        load_pred(1, 0, 2)
+        load_pred(1, 2, 4)
+        load_traits(0)
+        load_pred(2, 0, 4)
+        load_traits(1)
+        for q in range(4):
+            load_scales(q)
+        load_pred(3, 0, 4)
+        load_traits(2)
+        load_words(*W_CHUNKS[0])
+        load_traits(3)
+        for v0, v1 in W_CHUNKS[1:]:
+            load_words(v0, v1)
+
+        e_wide = keep.tile([P, 2, H, PACK, HALF], BF16, name="e_wide", align_bytes=64)
+        e_grp = keep.tile([P, 2, H, HALF, PACK], BF16, name="e_grp", align_bytes=64)
+        e_codes = keep.tile([P, 2, H, HALF], U32, name="e_codes", align_bytes=64)
+        e_sc = keep.tile([P, 2, H, HALF], U8, name="e_sc", align_bytes=64)
+        p_codes, p_sc, r_grp = [], [], []
+        for g in range(G):
+            pc = keep.tile([P, PACK, H, P], U32, name="p_codes%d" % g, align_bytes=64)
+            p_codes.append(pc)
+            ps = keep.tile([P, PACK, H, P], U8, name="p_sc%d" % g, align_bytes=64)
+            p_sc.append(ps)
+            rg = keep.tile([P, TRAITS, PACK], BF16, name="r_grp%d" % g, align_bytes=64)
+            r_grp.append(rg)
+        r_codes = keep.tile([P, G, TRAITS], U32, name="r_codes", align_bytes=64)
+        r_sc = keep.tile([P, G, TRAITS], U8, name="r_sc", align_bytes=64)
+        rstd = keep.tile([P, NV], F32, name="rstd")
+        rvar = keep.tile([P, NV], F32, name="rvar")
+
+        def eff_in(nh, h, t):
+            c0 = t * TRAITS + nh * HALF
+            return e_bytes[h][:, c0 : c0 + HALF].bitcast(FP8)
+
+        def widen_s(nh, h):
+            for t in range(PACK):
+                nc.scalar.activation(
+                    out=e_wide[:, nh, h, t, :],
+                    in_=eff_in(nh, h, t),
+                    func=ACT.Copy,
+                    scale=e_scale[:, h * PACK + t : h * PACK + t + 1],
+                )
+
+        def widen_v(nh, h):
+            for t in range(PACK):
+                nc.vector.tensor_scalar(
+                    out=e_wide[:, nh, h, t, :],
+                    in0=eff_in(nh, h, t),
+                    scalar1=e_scale[:, h * PACK + t : h * PACK + t + 1],
+                    scalar2=None,
+                    op0=ALU.mult,
+                )
+
+        def interleave(nh, h):
+            nc.vector.tensor_copy(
+                out=e_grp[:, nh, h, :, :], in_=e_wide[:, nh, h, :, :].rearrange("p t n -> p n t")
+            )
+
+        def quant_eff(nh):
+            nc.vector.quantize_mx(
+                out=e_codes[:, nh, :, :].rearrange("p h n -> p (h n)").bitcast(FP8X4),
+                scales=e_sc[:, nh, :, :].rearrange("p h n -> p (h n)"),
+                in_=e_grp[:, nh, :, :, :].rearrange("p h n t -> p (h n t)"),
+            )
+
+        p_grp = {}
+
+        def turn(g):
+            pg = work.tile([P, PACK, H, P, PACK], BF16, name="p_grp", bufs=2, align_bytes=64)
+            p_grp[g] = pg
+            for t in range(PACK):
+                words = p_raw[g][:, t, :].bitcast(F32)
+                bank = psum.tile([P, H, 2, P], F32, name="tp", bufs=3)
+                for h in range(H):
+                    for u in range(2):
+                        nc.tensor.transpose(
+                            bank[:, h, u, :], words[:, 256 * h + u : 256 * (h + 1) : 2], ident[:]
+                        )
+                dst = pg[:, t, :, :, :].rearrange("p h r j -> p (h r j)").bitcast(F32)
+                nc.scalar.copy(
+                    out=dst.rearrange("p (h r u) -> p h r u", h=H, u=2),
+                    in_=bank[:].rearrange("p h u r -> p h r u"),
+                )
+
+        def quant_pred(g, a):
+            ts = slice(2 * a, 2 * a + 2)
+            nc.vector.quantize_mx(
+                out=p_codes[g][:, ts, :, :].rearrange("p t h r -> p (t h r)").bitcast(FP8X4),
+                scales=p_sc[g][:, ts, :, :].rearrange("p t h r -> p (t h r)"),
+                in_=p_grp[g][:, ts, :, :, :].rearrange("p t h r j -> p (t h r j)"),
+            )
+
+        fit_bank = {}
+
+        def fit(g, c):
+            bank = psum.tile([P, PACK, P], F32, name="fit", bufs=2)
+            fit_bank[g, c] = bank
+            nh, n0 = c // 2, (c % 2) * P
+            for t in range(PACK):
+                for h in range(H):
+                    nc.tensor.matmul_mx(
+                        out=bank[:, t, :],
+                        lhsT=p_codes[g][:, t, h, :].bitcast(FP8X4),
+                        lhsT_scale=p_sc[g][:, t, h, :],
+                        rhs=e_codes[:, nh, h, n0 : n0 + P].bitcast(FP8X4),
+                        rhs_scale=e_sc[:, nh, h, n0 : n0 + P],
+                        start=(h == 0),
+                        stop=(h == H - 1),
+                    )
+
+        def resid(g, c):
+            cols = slice(c * P, (c + 1) * P)
+            nc.vector.tensor_tensor(
+                out=r_grp[g][:, cols, :],
+                in0=t_raw[g][:, :, cols].rearrange("p t n -> p n t"),
+                in1=fit_bank[g, c][:].rearrange("p t n -> p n t"),
+                op=ALU.subtract,
+            )
+
+        def quant_resid(g, a):
+            cols = slice(a * HALF, (a + 1) * HALF)
+            nc.vector.quantize_mx(
+                out=r_codes[:, g, cols].bitcast(FP8X4),
+                scales=r_sc[:, g, cols],
+                in_=r_grp[g][:, cols, :].rearrange("p n t -> p (n t)"),
+            )
+
+        score_bank = {}
+        bank_names = ("sc", "sc", "sc", "tp", "tp", "tp", "fit", "fit")
+        bank_bufs = {"sc": 3, "tp": 3, "fit": 2}
+
+        def score(v, g):
+            if g == 0:
+                which = bank_names[v % len(bank_names)]
+                bank = psum.tile([P, TRAITS], F32, name=which, bufs=bank_bufs[which])
+                score_bank[v] = bank
+            nc.tensor.matmul_mx(
+                out=score_bank[v][:],
+                lhsT=g_words[:, g, 2 * v * P : 2 * (v + 1) * P].bitcast(FP4X4),
+                lhsT_scale=g_scales[:, g * VARIANTS + v * P : g * VARIANTS + (v + 1) * P],
+                rhs=r_codes[:, g, :].bitcast(FP8X4),
+                rhs_scale=r_sc[:, g, :],
+                start=(g == 0),
+                stop=(g == G - 1),
+            )
+
+        def finish(v):
+            res = work.tile([P, TRAITS], F32, name="res", bufs=6)
+            parts = 2 if v == NV - 1 else 1
+            width = TRAITS // parts
+            for i in range(parts):
+                cols = slice(i * width, (i + 1) * width)
+                nc.scalar.activation(
+                    out=res[:, cols],
+                    in_=score_bank[v][:, cols],
+                    func=ACT.Square,
+                    scale=rstd[:, v : v + 1],
+                )
+                nc.sync.dma_start(out=out[v * P : (v + 1) * P, cols], in_=res[:, cols])
+
+        widen_s(0, 0)
+        widen_v(0, 1)
+        turn(0)
+        interleave(0, 1)
+        interleave(0, 0)
+        quant_pred(0, 0)
+        quant_eff(0)
+        quant_pred(0, 1)
+        widen_s(1, 0)
+        widen_v(1, 1)
+        turn(1)
+        fit(0, 0)
+        fit(0, 1)
+        interleave(1, 1)
+        interleave(1, 0)
+        resid(0, 0)
+        quant_eff(1)
+        resid(0, 1)
+        quant_pred(1, 0)
+        turn(2)
+        quant_pred(1, 1)
+        fit(0, 2)
+        fit(0, 3)
+        resid(0, 2)
+        quant_resid(0, 0)
+        resid(0, 3)
+        fit(1, 0)
+        fit(1, 1)
+        resid(1, 0)
+        quant_resid(0, 1)
+        resid(1, 1)
+        fit(1, 2)
+        fit(1, 3)
+        quant_pred(2, 0)
+        resid(1, 2)
+        quant_pred(2, 1)
+        resid(1, 3)
+        quant_resid(1, 0)
+        turn(3)
+        var_bank = psum.tile([P, P], BF16, name="tp", bufs=3)
+        nc.tensor.transpose(var_bank[:], var_rows[:], ident_b[:])
+        fit(2, 0)
+        fit(2, 1)
+        resid(2, 0)
+        quant_resid(1, 1)
+        resid(2, 1)
+        nc.vector.reciprocal(out=rvar[:], in_=var_bank[:, 0:NV])
+        nc.scalar.activation(out=rstd[:], in_=rvar[:], func=ACT.Sqrt)
+        fit(2, 2)
+        fit(2, 3)
+        quant_pred(3, 0)
+        resid(2, 2)
+        quant_pred(3, 1)
+        resid(2, 3)
+        quant_resid(2, 0)
+        for v in range(3):
+            score(v, 0)
+            score(v, 1)
+        fit(3, 0)
+        fit(3, 1)
+        resid(3, 0)
+        quant_resid(2, 1)
+        resid(3, 1)
+        fit(3, 2)
+        fit(3, 3)
+        resid(3, 2)
+        quant_resid(3, 0)
+        resid(3, 3)
+        quant_resid(3, 1)
+        for v in range(3, FIRST):
+            score(v, 0)
+            score(v, 1)
+        for v in range(FIRST):
+            score(v, 2)
+        for v in range(FIRST):
+            score(v, 3)
+            finish(v)
+        for v in range(FIRST, NV):
+            for g in range(G):
+                score(v, g)
+            finish(v)

@@ -25,7 +25,6 @@ H = PRED // K_PASS
 C = TRAITS // P
 NV = VARIANTS // P
 HALF = TRAITS // 2
-FIRST = 6
 W_CHUNKS = ((0, 6), (6, 12), (12, 18), (18, 24))
 
 
@@ -45,27 +44,31 @@ def tile_gwas_score_statistics_s13_kernel(
         make_identity(nc, ident_b[:])
         var_rows = keep.tile([P, P], BF16, name="var_rows")
         nc.gpsimd.memset(var_rows[:], 0.0)
-        g_scales = keep.tile([P, G * VARIANTS], U8, name="g_scales", align_bytes=64)
-        nc.gpsimd.memset(g_scales[:].bitcast(I32), 0)
+        zeros = keep.tile([P, TRAITS], BF16, name="zeros")
+        nc.vector.memset(zeros[:], 0.0)
         one = keep.tile([P, 1], F32, name="one")
         nc.vector.memset(one[:], 1.0)
-        root = keep.tile([P, 1], F32, name="root")
-        nc.scalar.activation(out=root[:], in_=one[:], func=ACT.Sqrt)
+        g_scales = keep.tile([P, G * VARIANTS], U8, name="g_scales", align_bytes=64)
+        nc.vector.memset(g_scales[:].bitcast(I32), 0)
 
         e_scale = keep.tile([P, H * PACK], F32, name="e_scale")
         nc.scalar.dma_start(
             out=e_scale[:].rearrange("p (h t) -> p h t", h=H),
             in_=eff_scale.rearrange("(h p t) o -> p h (t o)", p=P, t=PACK),
         )
-        nc.scalar.dma_start(out=var_rows[0:NV, :], in_=var.rearrange("(j p) -> j p", p=P))
+        root = keep.tile([P, 1], F32, name="root")
+        nc.scalar.activation(out=root[:], in_=one[:], func=ACT.Sqrt)
 
         e_bytes = []
         for h in range(H):
             eb = keep.tile([P, PACK * TRAITS], U8, name="e_bytes%d" % h, align_bytes=64)
-            nc.sync.dma_start(
-                out=eb[:], in_=eff_bytes.rearrange("(h p t) n -> h p (t n)", p=P, t=PACK)[h]
-            )
             e_bytes.append(eb)
+
+        def load_eff(h):
+            nc.sync.dma_start(
+                out=e_bytes[h][:],
+                in_=eff_bytes.rearrange("(h p t) n -> h p (t n)", p=P, t=PACK)[h],
+            )
 
         pred_v = pred.rearrange("(g p t) k -> g p t k", p=P, t=PACK)
         traits_v = traits.rearrange("(g p t) n -> g p t n", p=P, t=PACK)
@@ -102,17 +105,21 @@ def tile_gwas_score_statistics_s13_kernel(
             )
 
         load_pred(0, 0, 1)
+        load_eff(0)
+        load_eff(1)
         load_pred(0, 1, 2)
         load_pred(0, 2, 4)
         load_pred(1, 0, 2)
-        load_pred(1, 2, 4)
         load_traits(0)
-        load_pred(2, 0, 4)
+        load_pred(1, 2, 4)
+        load_pred(2, 0, 2)
+        load_pred(2, 2, 4)
         load_traits(1)
-        for q in range(4):
-            load_scales(q)
         load_pred(3, 0, 4)
         load_traits(2)
+        nc.sync.dma_start(out=var_rows[0:NV, :], in_=var.rearrange("(j p) -> j p", p=P))
+        for q in range(4):
+            load_scales(q)
         load_words(*W_CHUNKS[0])
         load_traits(3)
         for v0, v1 in W_CHUNKS[1:]:
@@ -158,8 +165,13 @@ def tile_gwas_score_statistics_s13_kernel(
                     op0=ALU.mult,
                 )
 
-        def interleave(nh, h):
+        def inter_v(nh, h):
             nc.vector.tensor_copy(
+                out=e_grp[:, nh, h, :, :], in_=e_wide[:, nh, h, :, :].rearrange("p t n -> p n t")
+            )
+
+        def inter_s(nh, h):
+            nc.scalar.copy(
                 out=e_grp[:, nh, h, :, :], in_=e_wide[:, nh, h, :, :].rearrange("p t n -> p n t")
             )
 
@@ -170,24 +182,47 @@ def tile_gwas_score_statistics_s13_kernel(
                 in_=e_grp[:, nh, :, :, :].rearrange("p h n t -> p (h n t)"),
             )
 
-        p_grp = {}
+        p_grp, turned, sorted_words = {}, {}, {}
 
-        def turn(g):
-            pg = work.tile([P, PACK, H, P, PACK], BF16, name="p_grp", bufs=2, align_bytes=64)
-            p_grp[g] = pg
-            for t in range(PACK):
-                words = p_raw[g][:, t, :].bitcast(F32)
-                bank = psum.tile([P, H, 2, P], F32, name="tp", bufs=3)
-                for h in range(H):
-                    for u in range(2):
-                        nc.tensor.transpose(
-                            bank[:, h, u, :], words[:, 256 * h + u : 256 * (h + 1) : 2], ident[:]
-                        )
-                dst = pg[:, t, :, :, :].rearrange("p h r j -> p (h r j)").bitcast(F32)
-                nc.scalar.copy(
-                    out=dst.rearrange("p (h r u) -> p h r u", h=H, u=2),
-                    in_=bank[:].rearrange("p h u r -> p h r u"),
+        def warm(n):
+            for i in range(n):
+                nc.tensor.matmul(
+                    warm_bank[:], lhsT=zeros[:, 0:P], rhs=zeros[:], start=True, stop=True
                 )
+
+        def sort_words(g, t):
+            if t == 0:
+                sw = work.tile([P, PACK, H, 2, P], F32, name="sorted_words", bufs=2)
+                sorted_words[g] = sw
+            words = p_raw[g][:, t, :].bitcast(F32)
+            nc.scalar.copy(
+                out=sorted_words[g][:, t, :, :, :],
+                in_=words.rearrange("p (h w u) -> p h u w", h=H, u=2),
+            )
+
+        def turn(g, t):
+            bank = psum.tile([P, H, 2, P], F32, name="tp", bufs=3)
+            turned[g, t] = bank
+            words = p_raw[g][:, t, :].bitcast(F32)
+            for h in range(H):
+                for u in range(2):
+                    if g in sorted_words:
+                        src = sorted_words[g][:, t, h, u, :]
+                    else:
+                        src = words[:, 256 * h + u : 256 * (h + 1) : 2]
+                    nc.tensor.transpose(bank[:, h, u, :], src, ident[:])
+
+        def take(g, t, on_vector=False):
+            if g not in p_grp:
+                pg = work.tile([P, PACK, H, P, PACK], BF16, name="p_grp", bufs=2, align_bytes=64)
+                p_grp[g] = pg
+            dst = p_grp[g][:, t, :, :, :].rearrange("p h r j -> p (h r j)").bitcast(F32)
+            dst = dst.rearrange("p (h r u) -> p h r u", h=H, u=2)
+            src = turned[g, t][:].rearrange("p h u r -> p h r u")
+            if on_vector:
+                nc.vector.tensor_copy(out=dst, in_=src)
+            else:
+                nc.scalar.copy(out=dst, in_=src)
 
         def quant_pred(g, a):
             ts = slice(2 * a, 2 * a + 2)
@@ -199,14 +234,15 @@ def tile_gwas_score_statistics_s13_kernel(
 
         fit_bank = {}
 
-        def fit(g, c):
-            bank = psum.tile([P, PACK, P], F32, name="fit", bufs=2)
-            fit_bank[g, c] = bank
+        def fit(g, c, ts=range(PACK)):
+            if (g, c) not in fit_bank:
+                bank = psum.tile([P, PACK, P], F32, name="fit", bufs=3)
+                fit_bank[g, c] = bank
             nh, n0 = c // 2, (c % 2) * P
-            for t in range(PACK):
+            for t in ts:
                 for h in range(H):
                     nc.tensor.matmul_mx(
-                        out=bank[:, t, :],
+                        out=fit_bank[g, c][:, t, :],
                         lhsT=p_codes[g][:, t, h, :].bitcast(FP8X4),
                         lhsT_scale=p_sc[g][:, t, h, :],
                         rhs=e_codes[:, nh, h, n0 : n0 + P].bitcast(FP8X4),
@@ -233,8 +269,8 @@ def tile_gwas_score_statistics_s13_kernel(
             )
 
         score_bank = {}
-        bank_names = ("sc", "sc", "sc", "tp", "tp", "tp", "fit", "fit")
-        bank_bufs = {"sc": 3, "tp": 3, "fit": 2}
+        bank_names = ("sc", "sc", "tp", "tp", "tp", "fit", "fit", "fit")
+        bank_bufs = {"sc": 2, "tp": 3, "fit": 3}
 
         def score(v, g):
             if g == 0:
@@ -265,84 +301,127 @@ def tile_gwas_score_statistics_s13_kernel(
                 )
                 nc.sync.dma_start(out=out[v * P : (v + 1) * P, cols], in_=res[:, cols])
 
-        widen_s(0, 0)
-        widen_v(0, 1)
-        turn(0)
-        interleave(0, 1)
-        interleave(0, 0)
+        warm_bank = psum.tile([P, TRAITS], F32, name="sc", bufs=2)
+        warm(7)
+        turn(0, 0)
+        warm(3)
+        widen_s(0, 1)
+        widen_v(0, 0)
+        turn(0, 1)
+        warm(2)
+        widen_v(1, 0)
+        widen_s(1, 1)
+        inter_v(0, 0)
+        take(0, 0, True)
+        inter_s(0, 1)
+        turn(0, 2)
+        take(0, 1, True)
+        turn(0, 3)
+        inter_v(1, 0)
+        take(0, 2)
         quant_pred(0, 0)
+        turn(1, 0)
+        warm(1)
+        take(0, 3)
         quant_eff(0)
+        turn(1, 1)
+        inter_s(1, 1)
         quant_pred(0, 1)
-        widen_s(1, 0)
-        widen_v(1, 1)
-        turn(1)
-        fit(0, 0)
-        fit(0, 1)
-        interleave(1, 1)
-        interleave(1, 0)
-        resid(0, 0)
+        fit(0, 0, (0, 1))
+        fit(0, 1, (0, 1))
+        take(1, 0, True)
+        take(1, 1)
         quant_eff(1)
-        resid(0, 1)
+        fit(0, 0, (2, 3))
+        fit(0, 1, (2, 3))
+        sort_words(2, 0)
+        sort_words(2, 1)
         quant_pred(1, 0)
-        turn(2)
+        turn(1, 2)
+        turn(1, 3)
+        resid(0, 0)
+        resid(0, 1)
+        sort_words(2, 2)
+        take(1, 2)
+        quant_resid(0, 0)
+        take(1, 3, True)
+        turn(2, 0)
+        sort_words(2, 3)
+        turn(2, 1)
+        take(2, 0)
         quant_pred(1, 1)
         fit(0, 2)
         fit(0, 3)
+        take(2, 1)
         resid(0, 2)
-        quant_resid(0, 0)
-        resid(0, 3)
+        quant_pred(2, 0)
         fit(1, 0)
+        sort_words(3, 0)
+        resid(0, 3)
+        sort_words(3, 1)
         fit(1, 1)
         resid(1, 0)
+        sort_words(3, 2)
         quant_resid(0, 1)
+        turn(2, 2)
+        turn(2, 3)
+        sort_words(3, 3)
         resid(1, 1)
         fit(1, 2)
+        take(2, 2)
         fit(1, 3)
-        quant_pred(2, 0)
-        resid(1, 2)
-        quant_pred(2, 1)
-        resid(1, 3)
         quant_resid(1, 0)
-        turn(3)
+        take(2, 3)
+        resid(1, 2)
+        turn(3, 0)
+        turn(3, 1)
+        quant_pred(2, 1)
+        take(3, 0)
+        resid(1, 3)
+        fit(2, 0)
+        take(3, 1)
+        fit(2, 1)
+        quant_resid(1, 1)
+        resid(2, 0)
+        turn(3, 2)
+        resid(2, 1)
+        turn(3, 3)
+        take(3, 2, True)
+        take(3, 3)
         var_bank = psum.tile([P, P], BF16, name="tp", bufs=3)
         nc.tensor.transpose(var_bank[:], var_rows[:], ident_b[:])
-        fit(2, 0)
-        fit(2, 1)
-        resid(2, 0)
-        quant_resid(1, 1)
-        resid(2, 1)
+        fit(2, 2)
+        quant_resid(2, 0)
+        fit(2, 3)
+        resid(2, 2)
         nc.vector.reciprocal(out=rvar[:], in_=var_bank[:, 0:NV])
         nc.scalar.activation(out=rstd[:], in_=rvar[:], func=ACT.Sqrt)
-        fit(2, 2)
-        fit(2, 3)
-        quant_pred(3, 0)
-        resid(2, 2)
-        quant_pred(3, 1)
         resid(2, 3)
-        quant_resid(2, 0)
-        for v in range(3):
+        quant_pred(3, 0)
+        quant_resid(2, 1)
+        quant_pred(3, 1)
+        for v in range(4):
             score(v, 0)
             score(v, 1)
         fit(3, 0)
         fit(3, 1)
         resid(3, 0)
-        quant_resid(2, 1)
         resid(3, 1)
+        for v in range(4):
+            score(v, 2)
         fit(3, 2)
+        quant_resid(3, 0)
         fit(3, 3)
         resid(3, 2)
-        quant_resid(3, 0)
         resid(3, 3)
         quant_resid(3, 1)
-        for v in range(3, FIRST):
-            score(v, 0)
-            score(v, 1)
-        for v in range(FIRST):
-            score(v, 2)
-        for v in range(FIRST):
+        for v in range(4, 6):
+            for g in range(3):
+                score(v, g)
+        for v in range(6):
             score(v, 3)
             finish(v)
-        for v in range(FIRST, NV):
+        for v in range(6, NV):
             for g in range(G):
                 score(v, g)
             finish(v)

@@ -22,7 +22,6 @@ PACK = 4
 K_PASS = P * PACK
 G = INDIV // K_PASS
 H = PRED // K_PASS
-C = TRAITS // P
 NV = VARIANTS // P
 HALF = TRAITS // 2
 W_CHUNKS = ((0, 6), (6, 12), (12, 18), (18, 24))
@@ -98,11 +97,10 @@ def tile_gwas_score_statistics_s13_kernel(
                 out=words_sb[:, :, cols], in_=words_v[:, :, cols].rearrange("g p n -> p g n")
             )
 
-        def load_scales(q):
-            nc.sync.dma_start(
-                out=scales_sb[32 * q : 32 * q + 4, :, :],
-                in_=scales_v[:, 4 * q : 4 * q + 4, :].rearrange("g q n -> q g n"),
-            )
+        scale_rows = scales_v.rearrange("g (q r) n -> r q g n", r=4)
+
+        def load_scales(r):
+            nc.sync.dma_start(out=scales_sb[r : P : 32, :, :], in_=scale_rows[r])
 
         load_pred(0, 0, 1)
         load_eff(0)
@@ -115,13 +113,14 @@ def tile_gwas_score_statistics_s13_kernel(
         load_pred(2, 0, 2)
         load_pred(2, 2, 4)
         load_traits(1)
-        load_pred(3, 0, 4)
+        load_pred(3, 0, 2)
+        load_pred(3, 2, 4)
         load_traits(2)
-        nc.sync.dma_start(out=var_rows[0:NV, :], in_=var.rearrange("(j p) -> j p", p=P))
-        for q in range(4):
-            load_scales(q)
-        load_words(*W_CHUNKS[0])
         load_traits(3)
+        nc.sync.dma_start(out=var_rows[0:NV, :], in_=var.rearrange("(j p) -> j p", p=P))
+        load_words(*W_CHUNKS[0])
+        for r in range(4):
+            load_scales(r)
         for v0, v1 in W_CHUNKS[1:]:
             load_words(v0, v1)
 
@@ -129,14 +128,12 @@ def tile_gwas_score_statistics_s13_kernel(
         e_grp = keep.tile([P, 2, H, HALF, PACK], BF16, name="e_grp", align_bytes=64)
         e_codes = keep.tile([P, 2, H, HALF], U32, name="e_codes", align_bytes=64)
         e_sc = keep.tile([P, 2, H, HALF], U8, name="e_sc", align_bytes=64)
-        p_codes, p_sc, r_grp = [], [], []
+        p_codes, p_sc = [], []
         for g in range(G):
             pc = keep.tile([P, PACK, H, P], U32, name="p_codes%d" % g, align_bytes=64)
             p_codes.append(pc)
             ps = keep.tile([P, PACK, H, P], U8, name="p_sc%d" % g, align_bytes=64)
             p_sc.append(ps)
-            rg = keep.tile([P, TRAITS, PACK], BF16, name="r_grp%d" % g, align_bytes=64)
-            r_grp.append(rg)
         r_codes = keep.tile([P, G, TRAITS], U32, name="r_codes", align_bytes=64)
         r_sc = keep.tile([P, G, TRAITS], U8, name="r_sc", align_bytes=64)
         rstd = keep.tile([P, NV], F32, name="rstd")
@@ -182,7 +179,7 @@ def tile_gwas_score_statistics_s13_kernel(
                 in_=e_grp[:, nh, :, :, :].rearrange("p h n t -> p (h n t)"),
             )
 
-        p_grp, turned, sorted_words = {}, {}, {}
+        p_grp, turned = {}, {}
 
         def warm(n):
             for i in range(n):
@@ -190,26 +187,13 @@ def tile_gwas_score_statistics_s13_kernel(
                     warm_bank[:], lhsT=zeros[:, 0:P], rhs=zeros[:], start=True, stop=True
                 )
 
-        def sort_words(g, t):
-            if t == 0:
-                sw = work.tile([P, PACK, H, 2, P], F32, name="sorted_words", bufs=2)
-                sorted_words[g] = sw
-            words = p_raw[g][:, t, :].bitcast(F32)
-            nc.scalar.copy(
-                out=sorted_words[g][:, t, :, :, :],
-                in_=words.rearrange("p (h w u) -> p h u w", h=H, u=2),
-            )
-
         def turn(g, t):
             bank = psum.tile([P, H, 2, P], F32, name="tp", bufs=3)
             turned[g, t] = bank
             words = p_raw[g][:, t, :].bitcast(F32)
             for h in range(H):
                 for u in range(2):
-                    if g in sorted_words:
-                        src = sorted_words[g][:, t, h, u, :]
-                    else:
-                        src = words[:, 256 * h + u : 256 * (h + 1) : 2]
+                    src = words[:, 256 * h + u : 256 * (h + 1) : 2]
                     nc.tensor.transpose(bank[:, h, u, :], src, ident[:])
 
         def take(g, t, on_vector=False):
@@ -232,33 +216,42 @@ def tile_gwas_score_statistics_s13_kernel(
                 in_=p_grp[g][:, ts, :, :, :].rearrange("p t h r j -> p (t h r j)"),
             )
 
-        fit_bank = {}
+        fit_bank, r_plain, r_grp = {}, {}, {}
 
-        def fit(g, c, ts=range(PACK)):
-            if (g, c) not in fit_bank:
-                bank = psum.tile([P, PACK, P], F32, name="fit", bufs=3)
-                fit_bank[g, c] = bank
-            nh, n0 = c // 2, (c % 2) * P
-            for t in ts:
+        def fit(g, t, nhs=None):
+            if (g, t) not in fit_bank:
+                bank = psum.tile([P, TRAITS], F32, name="fit", bufs=4)
+                fit_bank[g, t] = bank
+            for nh in range(2) if nhs is None else nhs:
                 for h in range(H):
                     nc.tensor.matmul_mx(
-                        out=fit_bank[g, c][:, t, :],
+                        out=fit_bank[g, t][:, nh * HALF : (nh + 1) * HALF],
                         lhsT=p_codes[g][:, t, h, :].bitcast(FP8X4),
                         lhsT_scale=p_sc[g][:, t, h, :],
-                        rhs=e_codes[:, nh, h, n0 : n0 + P].bitcast(FP8X4),
-                        rhs_scale=e_sc[:, nh, h, n0 : n0 + P],
+                        rhs=e_codes[:, nh, h, :].bitcast(FP8X4),
+                        rhs_scale=e_sc[:, nh, h, :],
                         start=(h == 0),
                         stop=(h == H - 1),
                     )
 
-        def resid(g, c):
-            cols = slice(c * P, (c + 1) * P)
+        def resid(g, t):
+            if g not in r_plain:
+                rp = work.tile([P, PACK, TRAITS], BF16, name="r_plain", bufs=3)
+                r_plain[g] = rp
             nc.vector.tensor_tensor(
-                out=r_grp[g][:, cols, :],
-                in0=t_raw[g][:, :, cols].rearrange("p t n -> p n t"),
-                in1=fit_bank[g, c][:].rearrange("p t n -> p n t"),
-                op=ALU.subtract,
+                out=r_plain[g][:, t, :], in0=t_raw[g][:, t, :], in1=fit_bank[g, t][:], op=ALU.subtract
             )
+
+        def inter_resid(g, a, on_vector=False):
+            if g not in r_grp:
+                rg = work.tile([P, TRAITS, PACK], BF16, name="r_grp", bufs=3, align_bytes=64)
+                r_grp[g] = rg
+            cols = slice(a * HALF, (a + 1) * HALF)
+            src = r_plain[g][:, :, cols].rearrange("p t n -> p n t")
+            if on_vector:
+                nc.vector.tensor_copy(out=r_grp[g][:, cols, :], in_=src)
+            else:
+                nc.scalar.copy(out=r_grp[g][:, cols, :], in_=src)
 
         def quant_resid(g, a):
             cols = slice(a * HALF, (a + 1) * HALF)
@@ -269,8 +262,8 @@ def tile_gwas_score_statistics_s13_kernel(
             )
 
         score_bank = {}
-        bank_names = ("sc", "sc", "tp", "tp", "tp", "fit", "fit", "fit")
-        bank_bufs = {"sc": 2, "tp": 3, "fit": 3}
+        bank_names = ("sc", "tp", "tp", "tp", "fit", "fit", "fit", "fit")
+        bank_bufs = {"sc": 1, "tp": 3, "fit": 4}
 
         def score(v, g):
             if g == 0:
@@ -301,127 +294,125 @@ def tile_gwas_score_statistics_s13_kernel(
                 )
                 nc.sync.dma_start(out=out[v * P : (v + 1) * P, cols], in_=res[:, cols])
 
-        warm_bank = psum.tile([P, TRAITS], F32, name="sc", bufs=2)
+        warm_bank = psum.tile([P, TRAITS], F32, name="sc", bufs=1)
         warm(7)
         turn(0, 0)
-        warm(3)
-        widen_s(0, 1)
-        widen_v(0, 0)
-        turn(0, 1)
+        widen_s(0, 0)
         warm(2)
-        widen_v(1, 0)
-        widen_s(1, 1)
-        inter_v(0, 0)
-        take(0, 0, True)
-        inter_s(0, 1)
-        turn(0, 2)
-        take(0, 1, True)
-        turn(0, 3)
-        inter_v(1, 0)
-        take(0, 2)
-        quant_pred(0, 0)
-        turn(1, 0)
+        widen_v(0, 1)
         warm(1)
-        take(0, 3)
+        take(0, 0)
+        turn(0, 1)
+        inter_v(0, 0)
+        widen_s(1, 1)
+        warm(2)
+        inter_v(0, 1)
+        turn(0, 2)
+        take(0, 1)
+        turn(0, 3)
         quant_eff(0)
+        widen_s(1, 0)
+        turn(1, 0)
+        take(0, 2, True)
+        warm(1)
+        quant_pred(0, 0)
         turn(1, 1)
-        inter_s(1, 1)
+        take(0, 3)
+        inter_v(1, 0)
+        take(1, 0)
+        fit(0, 0, (0,))
         quant_pred(0, 1)
-        fit(0, 0, (0, 1))
-        fit(0, 1, (0, 1))
-        take(1, 0, True)
+        inter_s(1, 1)
+        fit(0, 1, (0,))
+        fit(0, 2, (0,))
         take(1, 1)
+        fit(0, 3, (0,))
         quant_eff(1)
-        fit(0, 0, (2, 3))
-        fit(0, 1, (2, 3))
-        sort_words(2, 0)
-        sort_words(2, 1)
-        quant_pred(1, 0)
         turn(1, 2)
+        quant_pred(1, 0)
         turn(1, 3)
+        take(1, 2, True)
+        fit(0, 0, (1,))
+        take(1, 3)
+        fit(0, 1, (1,))
         resid(0, 0)
-        resid(0, 1)
-        sort_words(2, 2)
-        take(1, 2)
-        quant_resid(0, 0)
-        take(1, 3, True)
+        fit(0, 2, (1,))
+        fit(0, 3, (1,))
+        resid(0, 2)
         turn(2, 0)
-        sort_words(2, 3)
+        resid(0, 3)
         turn(2, 1)
         take(2, 0)
-        quant_pred(1, 1)
-        fit(0, 2)
-        fit(0, 3)
-        take(2, 1)
-        resid(0, 2)
-        quant_pred(2, 0)
+        resid(0, 1)
         fit(1, 0)
-        sort_words(3, 0)
-        resid(0, 3)
-        sort_words(3, 1)
+        take(2, 1)
+        quant_pred(1, 1)
         fit(1, 1)
-        resid(1, 0)
-        sort_words(3, 2)
-        quant_resid(0, 1)
-        turn(2, 2)
-        turn(2, 3)
-        sort_words(3, 3)
-        resid(1, 1)
+        inter_resid(0, 0)
+        quant_pred(2, 0)
         fit(1, 2)
-        take(2, 2)
+        resid(1, 1)
         fit(1, 3)
-        quant_resid(1, 0)
-        take(2, 3)
+        inter_resid(0, 1)
+        quant_resid(0, 0)
+        turn(2, 2)
         resid(1, 2)
-        turn(3, 0)
-        turn(3, 1)
-        quant_pred(2, 1)
-        take(3, 0)
-        resid(1, 3)
+        turn(2, 3)
+        take(2, 2)
+        quant_resid(0, 1)
         fit(2, 0)
-        take(3, 1)
+        resid(1, 0)
+        take(2, 3)
         fit(2, 1)
-        quant_resid(1, 1)
+        resid(1, 3)
+        turn(3, 0)
+        quant_pred(2, 1)
+        inter_resid(1, 0)
+        turn(3, 1)
         resid(2, 0)
-        turn(3, 2)
+        fit(2, 2)
         resid(2, 1)
+        take(3, 1)
+        fit(2, 3)
+        quant_resid(1, 0)
+        take(3, 0)
+        resid(2, 2)
+        turn(3, 2)
+        quant_pred(3, 0)
         turn(3, 3)
-        take(3, 2, True)
-        take(3, 3)
         var_bank = psum.tile([P, P], BF16, name="tp", bufs=3)
         nc.tensor.transpose(var_bank[:], var_rows[:], ident_b[:])
-        fit(2, 2)
-        quant_resid(2, 0)
-        fit(2, 3)
-        resid(2, 2)
+        take(3, 2)
+        inter_resid(1, 1, True)
+        fit(3, 0)
+        take(3, 3)
+        resid(2, 3)
+        fit(3, 1)
+        quant_pred(3, 1)
         nc.vector.reciprocal(out=rvar[:], in_=var_bank[:, 0:NV])
         nc.scalar.activation(out=rstd[:], in_=rvar[:], func=ACT.Sqrt)
-        resid(2, 3)
-        quant_pred(3, 0)
+        inter_resid(2, 1)
+        inter_resid(2, 0, True)
+        fit(3, 2)
+        fit(3, 3)
+        quant_resid(1, 1)
+        quant_resid(2, 0)
         quant_resid(2, 1)
-        quant_pred(3, 1)
-        for v in range(4):
-            score(v, 0)
-            score(v, 1)
-        fit(3, 0)
-        fit(3, 1)
         resid(3, 0)
         resid(3, 1)
-        for v in range(4):
-            score(v, 2)
-        fit(3, 2)
-        quant_resid(3, 0)
-        fit(3, 3)
         resid(3, 2)
         resid(3, 3)
+        inter_resid(3, 0)
+        inter_resid(3, 1)
+        quant_resid(3, 0)
         quant_resid(3, 1)
-        for v in range(4, 6):
+        for v in range(8):
             for g in range(3):
                 score(v, g)
-        for v in range(6):
+        for v in range(8):
             score(v, 3)
             finish(v)
-        for v in range(6, NV):
+        for v in range(8, NV):
             for g in range(G):
                 score(v, g)
             finish(v)

@@ -113,18 +113,18 @@ def tile_gwas_score_statistics_s13_kernel(
         load_pred(2, 0, 2)
         load_pred(2, 2, 4)
         load_traits(1)
+        nc.sync.dma_start(out=var_rows[0:NV, :], in_=var.rearrange("(j p) -> j p", p=P))
         load_pred(3, 0, 2)
         load_pred(3, 2, 4)
         load_traits(2)
         load_traits(3)
-        nc.sync.dma_start(out=var_rows[0:NV, :], in_=var.rearrange("(j p) -> j p", p=P))
         load_words(*W_CHUNKS[0])
         for r in range(4):
             load_scales(r)
         for v0, v1 in W_CHUNKS[1:]:
             load_words(v0, v1)
 
-        e_wide = keep.tile([P, 2, H, PACK, HALF], BF16, name="e_wide", align_bytes=64)
+        e_wide = keep.tile([P, H, PACK, TRAITS], BF16, name="e_wide", align_bytes=64)
         e_grp = keep.tile([P, 2, H, HALF, PACK], BF16, name="e_grp", align_bytes=64)
         e_codes = keep.tile([P, 2, H, HALF], U32, name="e_codes", align_bytes=64)
         e_sc = keep.tile([P, 2, H, HALF], U8, name="e_sc", align_bytes=64)
@@ -139,38 +139,27 @@ def tile_gwas_score_statistics_s13_kernel(
         rstd = keep.tile([P, NV], F32, name="rstd")
         rvar = keep.tile([P, NV], F32, name="rvar")
 
-        def eff_in(nh, h, t):
-            c0 = t * TRAITS + nh * HALF
-            return e_bytes[h][:, c0 : c0 + HALF].bitcast(FP8)
-
-        def widen_s(nh, h):
-            for t in range(PACK):
-                nc.scalar.activation(
-                    out=e_wide[:, nh, h, t, :],
-                    in_=eff_in(nh, h, t),
-                    func=ACT.Copy,
-                    scale=e_scale[:, h * PACK + t : h * PACK + t + 1],
-                )
-
-        def widen_v(nh, h):
-            for t in range(PACK):
+        def widen(h, t, on_vector=False):
+            raw = e_bytes[h][:, t * TRAITS : (t + 1) * TRAITS].bitcast(FP8)
+            scale = e_scale[:, h * PACK + t : h * PACK + t + 1]
+            if on_vector:
                 nc.vector.tensor_scalar(
-                    out=e_wide[:, nh, h, t, :],
-                    in0=eff_in(nh, h, t),
-                    scalar1=e_scale[:, h * PACK + t : h * PACK + t + 1],
-                    scalar2=None,
-                    op0=ALU.mult,
+                    out=e_wide[:, h, t, :], in0=raw, scalar1=scale, scalar2=None, op0=ALU.mult
                 )
+            else:
+                nc.scalar.activation(out=e_wide[:, h, t, :], in_=raw, func=ACT.Copy, scale=scale)
 
-        def inter_v(nh, h):
-            nc.vector.tensor_copy(
-                out=e_grp[:, nh, h, :, :], in_=e_wide[:, nh, h, :, :].rearrange("p t n -> p n t")
-            )
+        def interleave(dst, src, on_vector):
+            dst = dst.rearrange("p (c i) t -> p c t i", i=4)
+            src = src.rearrange("p t (c i) -> p c t i", i=4)
+            if on_vector:
+                nc.vector.tensor_copy(out=dst, in_=src)
+            else:
+                nc.scalar.copy(out=dst, in_=src)
 
-        def inter_s(nh, h):
-            nc.scalar.copy(
-                out=e_grp[:, nh, h, :, :], in_=e_wide[:, nh, h, :, :].rearrange("p t n -> p n t")
-            )
+        def inter_eff(nh, h, on_vector=False):
+            cols = slice(nh * HALF, (nh + 1) * HALF)
+            interleave(e_grp[:, nh, h, :, :], e_wide[:, h, :, cols], on_vector)
 
         def quant_eff(nh):
             nc.vector.quantize_mx(
@@ -208,19 +197,18 @@ def tile_gwas_score_statistics_s13_kernel(
             else:
                 nc.scalar.copy(out=dst, in_=src)
 
-        def quant_pred(g, a):
-            ts = slice(2 * a, 2 * a + 2)
+        def quant_pred(g, t0, t1):
             nc.vector.quantize_mx(
-                out=p_codes[g][:, ts, :, :].rearrange("p t h r -> p (t h r)").bitcast(FP8X4),
-                scales=p_sc[g][:, ts, :, :].rearrange("p t h r -> p (t h r)"),
-                in_=p_grp[g][:, ts, :, :, :].rearrange("p t h r j -> p (t h r j)"),
+                out=p_codes[g][:, t0:t1, :, :].rearrange("p t h r -> p (t h r)").bitcast(FP8X4),
+                scales=p_sc[g][:, t0:t1, :, :].rearrange("p t h r -> p (t h r)"),
+                in_=p_grp[g][:, t0:t1, :, :, :].rearrange("p t h r j -> p (t h r j)"),
             )
 
         fit_bank, r_plain, r_grp = {}, {}, {}
 
         def fit(g, t, nhs=None):
             if (g, t) not in fit_bank:
-                bank = psum.tile([P, TRAITS], F32, name="fit", bufs=4)
+                bank = psum.tile([P, TRAITS], F32, name="fit", bufs=3)
                 fit_bank[g, t] = bank
             for nh in range(2) if nhs is None else nhs:
                 for h in range(H):
@@ -247,14 +235,10 @@ def tile_gwas_score_statistics_s13_kernel(
                 rg = work.tile([P, TRAITS, PACK], BF16, name="r_grp", bufs=3, align_bytes=64)
                 r_grp[g] = rg
             cols = slice(a * HALF, (a + 1) * HALF)
-            src = r_plain[g][:, :, cols].rearrange("p t n -> p n t")
-            if on_vector:
-                nc.vector.tensor_copy(out=r_grp[g][:, cols, :], in_=src)
-            else:
-                nc.scalar.copy(out=r_grp[g][:, cols, :], in_=src)
+            interleave(r_grp[g][:, cols, :], r_plain[g][:, :, cols], on_vector)
 
-        def quant_resid(g, a):
-            cols = slice(a * HALF, (a + 1) * HALF)
+        def quant_resid(g, a0, a1):
+            cols = slice(a0 * HALF, a1 * HALF)
             nc.vector.quantize_mx(
                 out=r_codes[:, g, cols].bitcast(FP8X4),
                 scales=r_sc[:, g, cols],
@@ -262,8 +246,8 @@ def tile_gwas_score_statistics_s13_kernel(
             )
 
         score_bank = {}
-        bank_names = ("sc", "tp", "tp", "tp", "fit", "fit", "fit", "fit")
-        bank_bufs = {"sc": 1, "tp": 3, "fit": 4}
+        bank_names = ("sc", "sc", "tp", "tp", "tp", "fit", "fit", "fit")
+        bank_bufs = {"sc": 2, "tp": 3, "fit": 3}
 
         def score(v, g):
             if g == 0:
@@ -294,121 +278,117 @@ def tile_gwas_score_statistics_s13_kernel(
                 )
                 nc.sync.dma_start(out=out[v * P : (v + 1) * P, cols], in_=res[:, cols])
 
-        warm_bank = psum.tile([P, TRAITS], F32, name="sc", bufs=1)
-        warm(7)
+        warm_bank = psum.tile([P, TRAITS], F32, name="sc", bufs=2)
+        warm(5)
         turn(0, 0)
-        widen_s(0, 0)
-        warm(2)
-        widen_v(0, 1)
+        widen(0, 0, True)
+        widen(0, 1)
         warm(1)
+        widen(0, 3, True)
         take(0, 0)
+        widen(1, 1, True)
+        warm(1)
+        widen(1, 2, True)
+        widen(1, 3)
         turn(0, 1)
-        inter_v(0, 0)
-        widen_s(1, 1)
-        warm(2)
-        inter_v(0, 1)
+        widen(0, 2, True)
+        widen(1, 0, True)
         turn(0, 2)
+        inter_eff(0, 0, True)
         take(0, 1)
         turn(0, 3)
-        quant_eff(0)
-        widen_s(1, 0)
-        turn(1, 0)
+        inter_eff(0, 1)
         take(0, 2, True)
-        warm(1)
-        quant_pred(0, 0)
+        turn(1, 0)
+        quant_pred(0, 0, 2)
+        inter_eff(1, 1)
         turn(1, 1)
+        quant_eff(0)
         take(0, 3)
-        inter_v(1, 0)
-        take(1, 0)
+        inter_eff(1, 0, True)
         fit(0, 0, (0,))
-        quant_pred(0, 1)
-        inter_s(1, 1)
         fit(0, 1, (0,))
-        fit(0, 2, (0,))
-        take(1, 1)
-        fit(0, 3, (0,))
         quant_eff(1)
+        take(1, 0)
+        take(1, 1)
         turn(1, 2)
-        quant_pred(1, 0)
+        quant_pred(0, 2, 4)
         turn(1, 3)
         take(1, 2, True)
         fit(0, 0, (1,))
-        take(1, 3)
         fit(0, 1, (1,))
-        resid(0, 0)
-        fit(0, 2, (1,))
-        fit(0, 3, (1,))
-        resid(0, 2)
+        take(1, 3)
         turn(2, 0)
-        resid(0, 3)
+        resid(0, 0)
         turn(2, 1)
-        take(2, 0)
         resid(0, 1)
-        fit(1, 0)
+        take(2, 0)
+        fit(0, 2)
+        quant_pred(1, 0, 4)
         take(2, 1)
-        quant_pred(1, 1)
-        fit(1, 1)
-        inter_resid(0, 0)
-        quant_pred(2, 0)
-        fit(1, 2)
-        resid(1, 1)
-        fit(1, 3)
-        inter_resid(0, 1)
-        quant_resid(0, 0)
+        fit(0, 3)
         turn(2, 2)
-        resid(1, 2)
+        resid(0, 2)
         turn(2, 3)
         take(2, 2)
-        quant_resid(0, 1)
-        fit(2, 0)
-        resid(1, 0)
+        fit(1, 0)
+        resid(0, 3)
         take(2, 3)
-        fit(2, 1)
-        resid(1, 3)
+        fit(1, 1)
+        resid(1, 0)
+        inter_resid(0, 0)
         turn(3, 0)
-        quant_pred(2, 1)
-        inter_resid(1, 0)
+        quant_pred(2, 0, 4)
+        fit(1, 2)
+        inter_resid(0, 1)
         turn(3, 1)
-        resid(2, 0)
-        fit(2, 2)
-        resid(2, 1)
-        take(3, 1)
-        fit(2, 3)
-        quant_resid(1, 0)
-        take(3, 0)
-        resid(2, 2)
         turn(3, 2)
-        quant_pred(3, 0)
+        resid(1, 1)
+        take(3, 0)
+        fit(2, 0)
+        resid(1, 2)
+        take(3, 1)
+        fit(2, 1)
+        quant_resid(0, 0, 2)
+        take(3, 2)
         turn(3, 3)
         var_bank = psum.tile([P, P], BF16, name="tp", bufs=3)
         nc.tensor.transpose(var_bank[:], var_rows[:], ident_b[:])
-        take(3, 2)
-        inter_resid(1, 1, True)
-        fit(3, 0)
+        resid(2, 0)
+        fit(1, 3)
         take(3, 3)
-        resid(2, 3)
-        fit(3, 1)
-        quant_pred(3, 1)
+        resid(2, 1)
+        fit(2, 2)
+        resid(1, 3)
+        fit(2, 3)
+        quant_pred(3, 0, 4)
         nc.vector.reciprocal(out=rvar[:], in_=var_bank[:, 0:NV])
         nc.scalar.activation(out=rstd[:], in_=rvar[:], func=ACT.Sqrt)
-        inter_resid(2, 1)
-        inter_resid(2, 0, True)
-        fit(3, 2)
-        fit(3, 3)
-        quant_resid(1, 1)
-        quant_resid(2, 0)
-        quant_resid(2, 1)
+        inter_resid(1, 0)
+        inter_resid(1, 1)
+        resid(2, 2)
+        fit(3, 0)
+        resid(2, 3)
+        fit(3, 1)
         resid(3, 0)
+        fit(3, 2)
+        inter_resid(2, 0)
+        quant_resid(1, 0, 2)
+        fit(3, 3)
+        inter_resid(2, 1)
         resid(3, 1)
         resid(3, 2)
         resid(3, 3)
+        quant_resid(2, 0, 2)
         inter_resid(3, 0)
-        inter_resid(3, 1)
-        quant_resid(3, 0)
-        quant_resid(3, 1)
+        inter_resid(3, 1, True)
+        quant_resid(3, 1, 2)
+        quant_resid(3, 0, 1)
         for v in range(8):
-            for g in range(3):
-                score(v, g)
+            score(v, 0)
+            score(v, 1)
+        for v in range(8):
+            score(v, 2)
         for v in range(8):
             score(v, 3)
             finish(v)

from contextlib import ExitStack

import concourse.mybir as mybir
from concourse.masks import make_identity

INDIV, PRED, VARIANTS, TRAITS = 2048, 1024, 3072, 512
FLOPS = 2 * INDIV * PRED * TRAITS + 2 * INDIV * VARIANTS * TRAITS

F32 = mybir.dt.float32
BF16 = mybir.dt.bfloat16
I32 = mybir.dt.int32
U32 = mybir.dt.uint32
U8 = mybir.dt.uint8
FP8 = mybir.dt.float8_e4m3fn
FP8X4 = mybir.dt.float8_e4m3fn_x4
FP4X4 = mybir.dt.float4_e2m1fn_x4
ACT = mybir.ActivationFunctionType
ALU = mybir.AluOpType

P = 128
PACK = 4
K_PASS = P * PACK
G = INDIV // K_PASS
H = PRED // K_PASS
NV = VARIANTS // P
HALF = TRAITS // 2
W_CHUNKS = ((0, 6), (6, 12), (12, 18), (18, 24))


def tile_gwas_score_statistics_s13_kernel(
    tc, pred, eff_bytes, eff_scale, traits, geno_words, geno_scales, var, out
):
    nc = tc.nc
    with ExitStack() as ctx:
        keep = ctx.enter_context(tc.tile_pool(name="keep", bufs=1))
        work = ctx.enter_context(tc.tile_pool(name="work", bufs=3))
        psum = ctx.enter_context(tc.psum_pool(name="psum", bufs=2))
        ctx.enter_context(tc.manual_schedule())

        ident = keep.tile([P, P], F32, name="ident")
        make_identity(nc, ident[:])
        ident_b = keep.tile([P, P], BF16, name="ident_b")
        make_identity(nc, ident_b[:])
        var_rows = keep.tile([P, P], BF16, name="var_rows")
        nc.gpsimd.memset(var_rows[:], 0.0)
        zeros = keep.tile([P, TRAITS], BF16, name="zeros")
        nc.vector.memset(zeros[:], 0.0)
        one = keep.tile([P, 1], F32, name="one")
        nc.vector.memset(one[:], 1.0)
        g_scales = keep.tile([P, G * VARIANTS], U8, name="g_scales", align_bytes=64)
        nc.vector.memset(g_scales[:].bitcast(I32), 0)

        e_scale = keep.tile([P, H * PACK], F32, name="e_scale")
        nc.scalar.dma_start(
            out=e_scale[:].rearrange("p (h t) -> p h t", h=H),
            in_=eff_scale.rearrange("(h p t) o -> p h (t o)", p=P, t=PACK),
        )
        root = keep.tile([P, 1], F32, name="root")
        nc.scalar.activation(out=root[:], in_=one[:], func=ACT.Sqrt)

        e_bytes = []
        for h in range(H):
            eb = keep.tile([P, PACK * TRAITS], U8, name="e_bytes%d" % h, align_bytes=64)
            e_bytes.append(eb)

        def load_eff(h):
            nc.sync.dma_start(
                out=e_bytes[h][:],
                in_=eff_bytes.rearrange("(h p t) n -> h p (t n)", p=P, t=PACK)[h],
            )

        pred_v = pred.rearrange("(g p t) k -> g p t k", p=P, t=PACK)
        traits_v = traits.rearrange("(g p t) n -> g p t n", p=P, t=PACK)
        p_raw, t_raw = [], []
        for g in range(G):
            pr = keep.tile([P, PACK, PRED], BF16, name="p_raw%d" % g, align_bytes=64)
            p_raw.append(pr)
            tr = keep.tile([P, PACK, TRAITS], BF16, name="t_raw%d" % g, align_bytes=64)
            t_raw.append(tr)

        def load_pred(g, t0, t1):
            nc.sync.dma_start(out=p_raw[g][:, t0:t1, :], in_=pred_v[g, :, t0:t1, :])

        def load_traits(g):
            nc.sync.dma_start(out=t_raw[g][:], in_=traits_v[g])

        g_words = keep.tile([P, G, 2 * VARIANTS], U8, name="g_words", align_bytes=64)
        words_v = geno_words.bitcast(I32)
        words_flat = g_words[:].rearrange("p g n -> p (g n)").bitcast(I32)
        words_sb = words_flat.rearrange("p (g n) -> p g n", g=G)
        scales_v = geno_scales.bitcast(I32)
        scales_sb = g_scales[:].bitcast(I32).rearrange("p (g n) -> p g n", g=G)

        def load_words(v0, v1):
            cols = slice(v0 * P // 2, v1 * P // 2)
            nc.sync.dma_start(
                out=words_sb[:, :, cols], in_=words_v[:, :, cols].rearrange("g p n -> p g n")
            )

        scale_rows = scales_v.rearrange("g (q r) n -> r q g n", r=4)

        def load_scales(r):
            nc.sync.dma_start(out=scales_sb[r : P : 32, :, :], in_=scale_rows[r])

        load_pred(0, 0, 1)
        load_eff(0)
        load_eff(1)
        load_pred(0, 1, 2)
        load_pred(0, 2, 4)
        load_pred(1, 0, 2)
        load_traits(0)
        load_pred(1, 2, 4)
        load_pred(2, 0, 2)
        load_pred(2, 2, 4)
        load_traits(1)
        nc.sync.dma_start(out=var_rows[0:NV, :], in_=var.rearrange("(j p) -> j p", p=P))
        load_pred(3, 0, 2)
        load_pred(3, 2, 4)
        load_traits(2)
        load_traits(3)
        load_words(*W_CHUNKS[0])
        for r in range(4):
            load_scales(r)
        for v0, v1 in W_CHUNKS[1:]:
            load_words(v0, v1)

        e_wide = keep.tile([P, H, PACK, TRAITS], BF16, name="e_wide", align_bytes=64)
        e_grp = keep.tile([P, 2, H, HALF, PACK], BF16, name="e_grp", align_bytes=64)
        e_codes = keep.tile([P, 2, H, HALF], U32, name="e_codes", align_bytes=64)
        e_sc = keep.tile([P, 2, H, HALF], U8, name="e_sc", align_bytes=64)
        p_codes, p_sc = [], []
        for g in range(G):
            pc = keep.tile([P, PACK, H, P], U32, name="p_codes%d" % g, align_bytes=64)
            p_codes.append(pc)
            ps = keep.tile([P, PACK, H, P], U8, name="p_sc%d" % g, align_bytes=64)
            p_sc.append(ps)
        r_codes = keep.tile([P, G, TRAITS], U32, name="r_codes", align_bytes=64)
        r_sc = keep.tile([P, G, TRAITS], U8, name="r_sc", align_bytes=64)
        rstd = keep.tile([P, NV], F32, name="rstd")
        rvar = keep.tile([P, NV], F32, name="rvar")

        def widen(h, t, on_vector=False):
            raw = e_bytes[h][:, t * TRAITS : (t + 1) * TRAITS].bitcast(FP8)
            scale = e_scale[:, h * PACK + t : h * PACK + t + 1]
            if on_vector:
                nc.vector.tensor_scalar(
                    out=e_wide[:, h, t, :], in0=raw, scalar1=scale, scalar2=None, op0=ALU.mult
                )
            else:
                nc.scalar.activation(out=e_wide[:, h, t, :], in_=raw, func=ACT.Copy, scale=scale)

        def interleave(dst, src, on_vector):
            dst = dst.rearrange("p (c i) t -> p c t i", i=4)
            src = src.rearrange("p t (c i) -> p c t i", i=4)
            if on_vector:
                nc.vector.tensor_copy(out=dst, in_=src)
            else:
                nc.scalar.copy(out=dst, in_=src)

        def inter_eff(nh, h, on_vector=False):
            cols = slice(nh * HALF, (nh + 1) * HALF)
            interleave(e_grp[:, nh, h, :, :], e_wide[:, h, :, cols], on_vector)

        def quant_eff(nh):
            nc.vector.quantize_mx(
                out=e_codes[:, nh, :, :].rearrange("p h n -> p (h n)").bitcast(FP8X4),
                scales=e_sc[:, nh, :, :].rearrange("p h n -> p (h n)"),
                in_=e_grp[:, nh, :, :, :].rearrange("p h n t -> p (h n t)"),
            )

        p_grp, turned = {}, {}

        def warm(n):
            for i in range(n):
                nc.tensor.matmul(
                    warm_bank[:], lhsT=zeros[:, 0:P], rhs=zeros[:], start=True, stop=True
                )

        def turn(g, t):
            bank = psum.tile([P, H, 2, P], F32, name="tp", bufs=3)
            turned[g, t] = bank
            words = p_raw[g][:, t, :].bitcast(F32)
            for h in range(H):
                for u in range(2):
                    src = words[:, 256 * h + u : 256 * (h + 1) : 2]
                    nc.tensor.transpose(bank[:, h, u, :], src, ident[:])

        def take(g, t, on_vector=False):
            if g not in p_grp:
                pg = work.tile([P, PACK, H, P, PACK], BF16, name="p_grp", bufs=2, align_bytes=64)
                p_grp[g] = pg
            dst = p_grp[g][:, t, :, :, :].rearrange("p h r j -> p (h r j)").bitcast(F32)
            dst = dst.rearrange("p (h r u) -> p h r u", h=H, u=2)
            src = turned[g, t][:].rearrange("p h u r -> p h r u")
            if on_vector:
                nc.vector.tensor_copy(out=dst, in_=src)
            else:
                nc.scalar.copy(out=dst, in_=src)

        def quant_pred(g, t0, t1):
            nc.vector.quantize_mx(
                out=p_codes[g][:, t0:t1, :, :].rearrange("p t h r -> p (t h r)").bitcast(FP8X4),
                scales=p_sc[g][:, t0:t1, :, :].rearrange("p t h r -> p (t h r)"),
                in_=p_grp[g][:, t0:t1, :, :, :].rearrange("p t h r j -> p (t h r j)"),
            )

        fit_bank, r_plain, r_grp = {}, {}, {}

        def fit(g, t, nhs=None):
            if (g, t) not in fit_bank:
                bank = psum.tile([P, TRAITS], F32, name="fit", bufs=3)
                fit_bank[g, t] = bank
            for nh in range(2) if nhs is None else nhs:
                for h in range(H):
                    nc.tensor.matmul_mx(
                        out=fit_bank[g, t][:, nh * HALF : (nh + 1) * HALF],
                        lhsT=p_codes[g][:, t, h, :].bitcast(FP8X4),
                        lhsT_scale=p_sc[g][:, t, h, :],
                        rhs=e_codes[:, nh, h, :].bitcast(FP8X4),
                        rhs_scale=e_sc[:, nh, h, :],
                        start=(h == 0),
                        stop=(h == H - 1),
                    )

        def resid(g, t):
            if g not in r_plain:
                rp = work.tile([P, PACK, TRAITS], BF16, name="r_plain", bufs=3)
                r_plain[g] = rp
            nc.vector.tensor_tensor(
                out=r_plain[g][:, t, :], in0=t_raw[g][:, t, :], in1=fit_bank[g, t][:], op=ALU.subtract
            )

        def inter_resid(g, a, on_vector=False):
            if g not in r_grp:
                rg = work.tile([P, TRAITS, PACK], BF16, name="r_grp", bufs=3, align_bytes=64)
                r_grp[g] = rg
            cols = slice(a * HALF, (a + 1) * HALF)
            interleave(r_grp[g][:, cols, :], r_plain[g][:, :, cols], on_vector)

        def quant_resid(g, a0, a1):
            cols = slice(a0 * HALF, a1 * HALF)
            nc.vector.quantize_mx(
                out=r_codes[:, g, cols].bitcast(FP8X4),
                scales=r_sc[:, g, cols],
                in_=r_grp[g][:, cols, :].rearrange("p n t -> p (n t)"),
            )

        score_bank = {}
        bank_names = ("sc", "sc", "tp", "tp", "tp", "fit", "fit", "fit")
        bank_bufs = {"sc": 2, "tp": 3, "fit": 3}

        def score(v, g):
            if g == 0:
                which = bank_names[v % len(bank_names)]
                bank = psum.tile([P, TRAITS], F32, name=which, bufs=bank_bufs[which])
                score_bank[v] = bank
            nc.tensor.matmul_mx(
                out=score_bank[v][:],
                lhsT=g_words[:, g, 2 * v * P : 2 * (v + 1) * P].bitcast(FP4X4),
                lhsT_scale=g_scales[:, g * VARIANTS + v * P : g * VARIANTS + (v + 1) * P],
                rhs=r_codes[:, g, :].bitcast(FP8X4),
                rhs_scale=r_sc[:, g, :],
                start=(g == 0),
                stop=(g == G - 1),
            )

        def finish(v):
            res = work.tile([P, TRAITS], F32, name="res", bufs=6)
            parts = 2 if v == NV - 1 else 1
            width = TRAITS // parts
            for i in range(parts):
                cols = slice(i * width, (i + 1) * width)
                nc.scalar.activation(
                    out=res[:, cols],
                    in_=score_bank[v][:, cols],
                    func=ACT.Square,
                    scale=rstd[:, v : v + 1],
                )
                nc.sync.dma_start(out=out[v * P : (v + 1) * P, cols], in_=res[:, cols])

        warm_bank = psum.tile([P, TRAITS], F32, name="sc", bufs=2)
        warm(5)
        turn(0, 0)
        widen(0, 0, True)
        widen(0, 1)
        warm(1)
        widen(0, 3, True)
        take(0, 0)
        widen(1, 1, True)
        warm(1)
        widen(1, 2, True)
        widen(1, 3)
        turn(0, 1)
        widen(0, 2, True)
        widen(1, 0, True)
        turn(0, 2)
        inter_eff(0, 0, True)
        take(0, 1)
        turn(0, 3)
        inter_eff(0, 1)
        take(0, 2, True)
        turn(1, 0)
        quant_pred(0, 0, 2)
        inter_eff(1, 1)
        turn(1, 1)
        quant_eff(0)
        take(0, 3)
        inter_eff(1, 0, True)
        fit(0, 0, (0,))
        fit(0, 1, (0,))
        quant_eff(1)
        take(1, 0)
        take(1, 1)
        turn(1, 2)
        quant_pred(0, 2, 4)
        turn(1, 3)
        take(1, 2, True)
        fit(0, 0, (1,))
        fit(0, 1, (1,))
        take(1, 3)
        turn(2, 0)
        resid(0, 0)
        turn(2, 1)
        resid(0, 1)
        take(2, 0)
        fit(0, 2)
        quant_pred(1, 0, 4)
        take(2, 1)
        fit(0, 3)
        turn(2, 2)
        resid(0, 2)
        turn(2, 3)
        take(2, 2)
        fit(1, 0)
        resid(0, 3)
        take(2, 3)
        fit(1, 1)
        resid(1, 0)
        inter_resid(0, 0)
        turn(3, 0)
        quant_pred(2, 0, 4)
        fit(1, 2)
        inter_resid(0, 1)
        turn(3, 1)
        turn(3, 2)
        resid(1, 1)
        take(3, 0)
        fit(2, 0)
        resid(1, 2)
        take(3, 1)
        fit(2, 1)
        quant_resid(0, 0, 2)
        take(3, 2)
        turn(3, 3)
        var_bank = psum.tile([P, P], BF16, name="tp", bufs=3)
        nc.tensor.transpose(var_bank[:], var_rows[:], ident_b[:])
        resid(2, 0)
        fit(1, 3)
        take(3, 3)
        resid(2, 1)
        fit(2, 2)
        resid(1, 3)
        fit(2, 3)
        quant_pred(3, 0, 4)
        nc.vector.reciprocal(out=rvar[:], in_=var_bank[:, 0:NV])
        nc.scalar.activation(out=rstd[:], in_=rvar[:], func=ACT.Sqrt)
        inter_resid(1, 0)
        inter_resid(1, 1)
        resid(2, 2)
        fit(3, 0)
        resid(2, 3)
        fit(3, 1)
        resid(3, 0)
        fit(3, 2)
        inter_resid(2, 0)
        quant_resid(1, 0, 2)
        fit(3, 3)
        inter_resid(2, 1)
        resid(3, 1)
        resid(3, 2)
        resid(3, 3)
        quant_resid(2, 0, 2)
        inter_resid(3, 0)
        inter_resid(3, 1, True)
        quant_resid(3, 1, 2)
        quant_resid(3, 0, 1)
        for v in range(8):
            score(v, 0)
            score(v, 1)
        for v in range(8):
            score(v, 2)
        for v in range(8):
            score(v, 3)
            finish(v)
        for v in range(8, NV):
            for g in range(G):
                score(v, g)
            finish(v)
